import numpy as np, ml_dtypes
CORES = [37,45,53,61,69,109,117,125]
N = 8
import mx_ref
NC, G = 128, 4
EPS = 0.001
BF = ml_dtypes.bfloat16
def cut(t, i, w=512):
    return t[:, w * i:w * i + w]
def tile(rs):
    return np.stack(rs, axis=2).reshape(128, -1).astype(BF)
def layer(w, X):
    out = []
    for i in range(G):
        for t in range(len(X)):
            p = mx_ref.matmul(mx_ref.quantize(cut(w, len(X) * i + t)), X[t])
            z = p if t == 0 else z + p
        out.append(z)
    return out
def normed(Z, s):
    return [z * f for z, f in zip(Z, s)]
def setup_inputs(rng):
    def f(*shape):
        return mx_ref.flush((rng.standard_normal(shape, dtype=np.float32) * np.exp2(rng.integers(-2, 3, shape[:-1] + (1,)))).astype(BF))
    return {"x": f(N, 128, 4 * NC), "w1": f(N, 128, G * 512), "w2": f(N, 128, 2 * 512)}
def setup_inputs_blocks(rng):
    d = setup_inputs(rng)
    for k in ("x", "w1", "w2"): d[k] = mx_ref.spread(d[k], rng, 4)
    return d
def setup_inputs_wide(rng):
    d = setup_inputs(rng)
    for k in ("x", "w1", "w2"): d[k] = mx_ref.flush((d[k].astype(np.float32) * np.exp2(rng.integers(-5, 6, (N, 1, 1))).astype(np.float32)).astype(BF))
    return d
def setup_inputs_rows(rng):
    d = setup_inputs(rng); v = d["w1"].astype(np.float32).reshape(N, 128, -1, 4)
    d["w1"] = mx_ref.flush((v * np.exp2(rng.integers(-6, 7, (N, 1, v.shape[2], 1))).astype(np.float32)).reshape(d["w1"].shape).astype(BF))
    return d
def setup_inputs_faint(rng):
    d = setup_inputs(rng); d["x"] = mx_ref.flush((d["x"].astype(np.float32) * np.float32(2.0 ** -12)).astype(BF))
    return d
def reference(x, w1, w2, own=None):
    Z = [layer(w1[r], [mx_ref.quantize(x[r])]) for r in range(N)]
    ms = [sum((Z[r][i].astype(np.float64) ** 2).sum(axis=1, keepdims=True) for r in range(N)) / (N * NC) for i in range(G)]
    s = [(1 / np.sqrt(m + EPS)).astype(np.float32) for m in ms]
    h = np.stack([tile(normed(Z[r], s)) for r in range(N)])
    use = h if own is None else own["h"]
    H = [mx_ref.quantize(use[j]) for j in range(N)]
    y = np.zeros((N, 128, NC), np.float32)
    for r in range(N):
        y[r] = mx_ref.matmul(mx_ref.quantize(cut(w2[r], 0)), H[r]) + mx_ref.matmul(mx_ref.quantize(cut(w2[r], 1)), H[(r + 1) % N])
    return {"h": h, "y": y}

@@ -1,0 +1,234 @@
+import math
+from concourse.bass import DstId, RemoteDMATransfer
+from concourse.mybir import dt, AluOpType, ActivationFunctionType
+
+NC, G, EPS = 128, 4, 0.001
+TW = 4 * NC
+
+SCRATCH = {
+    "xb": ("sbuf", [128, TW], "bfloat16"),
+    "w1b": ("sbuf", [128, G * TW], "bfloat16"),
+    "w2b": ("sbuf", [128, 2 * TW], "bfloat16"),
+    "hb": ("sbuf", [128, TW], "bfloat16"),
+    "xq": ("sbuf", [128, NC], "float8_e4m3fn_x4"), "xs": ("sbuf", [128, NC], "uint8"),
+    "w1q": ("sbuf", [128, G * 128], "float8_e4m3fn_x4"), "w1s": ("sbuf", [128, G * 128], "uint8"),
+    "w2q": ("sbuf", [128, 2 * 128], "float8_e4m3fn_x4"), "w2s": ("sbuf", [128, 2 * 128], "uint8"),
+    "hq": ("sbuf", [128, NC], "float8_e4m3fn_x4"), "hs": ("sbuf", [128, NC], "uint8"),
+    "nq": ("sbuf", [128, NC], "float8_e4m3fn_x4"), "ns": ("sbuf", [128, NC], "uint8"),
+    "z": ("psum", [128, G * 512], "float32"),
+    "yp": ("psum", [128, 512], "float32"),
+    "sqr": ("sbuf", [128, G * NC], "float32"),
+    "ssA": ("sbuf", [128, 4], "float32"), "ssB": ("sbuf", [128, 4], "float32"),
+    "hlA": ("sbuf", [128, 4], "float32"), "hlB": ("sbuf", [128, 12], "float32"),
+    "leA": ("sbuf", [128, 4], "float32"), "loA": ("sbuf", [128, 4], "float32"),
+    "leB": ("sbuf", [128, 4], "float32"), "loB": ("sbuf", [128, 4], "float32"),
+    "tA": ("sbuf", [128, 4], "float32"), "tB": ("sbuf", [128, 4], "float32"),
+    "aA": ("sbuf", [128, 4], "float32"), "aB": ("sbuf", [128, 4], "float32"),
+    "ia": ("sbuf", [128, 4], "float32"), "rt": ("sbuf", [128, 4], "float32"),
+    "s0": ("sbuf", [128, 4], "float32"), "u": ("sbuf", [128, 4], "float32"),
+    "v": ("sbuf", [128, 4], "float32"), "s1": ("sbuf", [128, 4], "float32"),
+    "yb": ("sbuf", [128, NC], "float32"),
+}
+SEMAPHORES = (["lx", "lv0", "lv1", "qx", "qv0", "qv1", "qh", "my", "sqA", "sqB", "hA", "hB", "eA", "oA", "eB", "oB",
+               "cc", "cs", "locA", "locB", "locC", "ktA", "kaA", "kiA", "krA", "ktB", "kaB", "kiB", "krB",
+               "n0", "n1", "n2", "n3", "sc", "cy", "sh", "sy"]
+              + ["lw%d" % i for i in range(G)] + ["qw%d" % i for i in range(G)] + ["m%d" % i for i in range(G)])
+
+
+def _count(mask):
+    return bin(mask).count("1")
+
+
+def _plan(T, topo):
+    cores = [int(c) for c in T.cores]
+    n = len(cores)
+    chips = [topo.chip(c) for c in cores]
+    near = [r for r in range(n) if r == 0 or topo.same_plane(chips[0], chips[r])]
+    far = [r for r in range(n) if r not in near]
+    plane = [near if r in near else far for r in range(n)]
+    partner, left = {}, list(far)
+    for r in near:
+        for q in left:
+            if topo.mates(chips[r], chips[q]):
+                partner[r], partner[q] = q, r
+                left.remove(q)
+                break
+    for r in near:
+        if r not in partner:
+            q = left.pop(0)
+            partner[r], partner[q] = q, r
+    port = []
+    for r in range(n):
+        goals = (cores[partner[r]], cores[(r - 1) % n])
+        cand = [k for k in range(topo.CHIPS * topo.CORES_PER_CHIP)
+                if topo.chip(k) == chips[r] and k not in cores and all(topo.may_write(k, d) for d in goals)]
+        cand.sort(key=lambda k: (topo.die(k) != topo.die(cores[r]), k))
+        port.append(cand[0])
+    return cores, plane, partner, port
+
+
+def _dst(topo, c):
+    rid, pid, _ = topo.addr(c)
+    return DstId(rid=rid, pnc=pid)
+
+
+def _send(g, topo, src, dst, out_ap, in_ap, rsem, lsem):
+    rid, pid, _ = topo.addr(dst)
+    m = topo.mask(src, dst)
+    g.remote_dma(out_ap=out_ap, in_ap=in_ap, remote_sem=rsem, local_sem=lsem, pid=pid, routing_id=rid,
+                 dma_engine_mask=m)
+    return _count(m)
+
+
+def _port_program(g, core, T, topo, r, cores, plane, partner, port):
+    S = T.sem
+    mine, other = cores[r], cores[partner[r]]
+    lo = topo.mask(core, other)
+    hi = topo.mask(core, mine) & ~lo
+    due = 0
+    for q in plane[r]:
+        out = topo.mask(cores[q], port[[p for p in plane[r] if p != q][0]])
+        due += _count(topo.mask(cores[q], core) & ~out) if q == r else _count(out)
+    left = 0
+    for land, w, asem, esem, osem, le, lo_buf in ((T.hlA, 1, S.hA, S.eA, S.oA, T.leA, T.loA),
+                                                  (T.hlB, 3, S.hB, S.eB, S.oB, T.leB, T.loB)):
+        srcs = [land[:, w * j:w * j + w] for j in range(len(plane[r]))]
+        g.wait_ge(asem, due)
+        g.remote_dma_fused([
+            RemoteDMATransfer(dst_ids=[_dst(topo, other)], dma_engine_mask=lo, remote_sem=osem, srcs=srcs,
+                              dsts=[lo_buf[:, 0:w]], alu_op=1),
+            RemoteDMATransfer(dst_ids=[_dst(topo, mine)], dma_engine_mask=hi, remote_sem=esem, srcs=srcs,
+                              dsts=[le[:, 0:w]], alu_op=1),
+        ], local_sem=S.locA)
+        left += _count(lo) + _count(hi)
+    goal = cores[(r - 1) % len(cores)]
+    got = _count(topo.mask(mine, core))
+    g.wait_ge(S.cc, got)
+    left += _send(g, topo, core, goal, T.nq[:].bitcast(dt.uint8), T.nq[:].bitcast(dt.uint8), S.cc, S.locA)
+    g.wait_ge(S.cs, got)
+    left += _send(g, topo, core, goal, T.ns[:], T.ns[:], S.cs, S.locA)
+    g.wait_ge(S.locA, left)
+
+
+def _rank_program(g, core, T, topo, r, cores, plane, partner, port):
+    S = T.sem
+    A, F = AluOpType, ActivationFunctionType
+    n = len(cores)
+    V, E, C, Y = g.vector, g.tensor, g.scalar, g.sync
+    my_port = port[r]
+    slot = plane[r].index(r)
+    away = [port[q] for q in plane[r] if q != r]
+    lo = topo.mask(core, away[0])
+    hi = topo.mask(core, my_port) & ~lo
+
+    def w1t(i):
+        return T.w1b[:, TW * i:TW * i + TW]
+
+    Y.dma_start(T.xb[:], T.x[:]).then_inc(S.lx, 16)
+    for i in range(G):
+        q = C if i % 2 == 0 else Y
+        q.dma_start(w1t(i), T.w1[:, TW * i:TW * i + TW]).then_inc(S["lw%d" % i], 16)
+
+    V.wait_ge(S.lx, 16)
+    V.quantize_mx(T.xq[:], T.xs[:], T.xb[:]).then_inc(S.qx, 1)
+    E.wait_ge(S.qx, 1)
+    for i in range(G):
+        cq, cs = T.w1q[:, 128 * i:128 * i + 128], T.w1s[:, 128 * i:128 * i + 128]
+        V.wait_ge(S["lw%d" % i], 16)
+        V.quantize_mx(cq, cs, w1t(i)).then_inc(S["qw%d" % i], 1)
+        E.wait_ge(S["qw%d" % i], 1)
+        E.matmul_mx(T.z[:, 512 * i:512 * i + NC], cq, cs, T.xq[:], T.xs[:], True, True).then_inc(S["m%d" % i], 1)
+        C.wait_ge(S["m%d" % i], 1)
+        acc = T.ssA[:, 0:1] if i == 0 else T.ssB[:, i - 1:i]
+        C.activation(T.sqr[:, NC * i:NC * i + NC], T.z[:, 512 * i:512 * i + NC], F.Square,
+                     scale=1.0 / math.sqrt(n * NC), accum_out=acc).then_inc(S.sqA if i == 0 else S.sqB, 1)
+
+    for src, land, w, ready, cnt, asem, lsem in ((T.ssA, T.hlA, 1, S.sqA, 1, S.hA, S.locA),
+                                                 (T.ssB, T.hlB, 3, S.sqB, G - 1, S.hB, S.locB)):
+        g.wait_ge(ready, cnt)
+        d = land[:, w * slot:w * slot + w]
+        g.remote_dma_fused([
+            RemoteDMATransfer(dst_ids=[_dst(topo, k) for k in away], dma_engine_mask=lo, remote_sem=asem,
+                              srcs=[src[:, 0:w]], dsts=[d for _ in away], alu_op=0),
+            RemoteDMATransfer(dst_ids=[_dst(topo, my_port)], dma_engine_mask=hi, remote_sem=asem,
+                              srcs=[src[:, 0:w]], dsts=[d], alu_op=0),
+        ], local_sem=lsem)
+    part = _count(lo) + _count(hi)
+
+    p_lo = topo.mask(port[partner[r]], core)
+    p_hi = topo.mask(my_port, core) & ~topo.mask(my_port, cores[partner[r]])
+    for le, lob, t, a, c0, w, es, os_, kt, ka, ki, kr in (
+            (T.leA, T.loA, T.tA, T.aA, 0, 1, S.eA, S.oA, S.ktA, S.kaA, S.kiA, S.krA),
+            (T.leB, T.loB, T.tB, T.aB, 1, 3, S.eB, S.oB, S.ktB, S.kaB, S.kiB, S.krB)):
+        V.wait_ge(es, _count(p_hi))
+        V.tensor_scalar(t[:, 0:w], le[:, 0:w], EPS, None, A.add).then_inc(kt, 1)
+        V.wait_ge(os_, _count(p_lo))
+        V.wait_ge(kt, 1)
+        V.tensor_tensor(a[:, 0:w], t[:, 0:w], lob[:, 0:w], A.add).then_inc(ka, 1)
+        C.wait_ge(ka, 1)
+        C.activation(T.rt[:, c0:c0 + w], a[:, 0:w], F.Sqrt).then_inc(kr, 1)
+        V.wait_ge(ka, 1)
+        V.reciprocal(T.ia[:, c0:c0 + w], a[:, 0:w]).then_inc(ki, 1)
+
+    for k in (S.kiA, S.kiB, S.krA, S.krB):
+        V.wait_ge(k, 1)
+    V.tensor_tensor(T.s0[:], T.rt[:], T.ia[:], A.mult).then_inc(S.n0, 1)
+    V.wait_ge(S.n0, 1)
+    V.tensor_tensor(T.u[:], T.rt[:], T.s0[:], A.mult).then_inc(S.n1, 1)
+    V.wait_ge(S.n1, 1)
+    V.tensor_scalar(T.v[:], T.u[:], -0.5, 1.5, A.mult, A.add).then_inc(S.n2, 1)
+    V.wait_ge(S.n2, 1)
+    V.tensor_tensor(T.s1[:], T.s0[:], T.v[:], A.mult).then_inc(S.n3, 1)
+
+    V.wait_ge(S.n3, 1)
+    V.wait_ge(S.sqA, 1)
+    V.wait_ge(S.sqB, G - 1)
+    C.wait_ge(S.n3, 1)
+    for b in range(G):
+        out, zb, col = T.hb[:, b:TW:4], T.z[:, 512 * b:512 * b + NC], T.s1[:, b:b + 1]
+        if b < G // 2:
+            V.tensor_scalar(out, zb, col, None, A.mult).then_inc(S.sc, 1)
+        else:
+            C.activation(out, zb, F.Identity, scale=col).then_inc(S.sc, 1)
+    V.wait_ge(S.sc, G)
+    V.quantize_mx(T.hq[:], T.hs[:], T.hb[:]).then_inc(S.qh, 1)
+
+    g.wait_ge(S.qh, 1)
+    gone = _send(g, topo, core, my_port, T.nq[:].bitcast(dt.uint8), T.hq[:].bitcast(dt.uint8), S.cc, S.locC)
+    gone += _send(g, topo, core, my_port, T.ns[:], T.hs[:], S.cs, S.locC)
+    g.wait_ge(S.locA, part)
+
+    Y.wait_ge(S.locB, part)
+    Y.dma_start(T.w2b[:, 0:TW], T.w2[:, 0:TW]).then_inc(S.lv0, 16)
+    Y.wait_ge(S.locC, gone)
+    Y.dma_start(T.w2b[:, TW:2 * TW], T.w2[:, TW:2 * TW]).then_inc(S.lv1, 16)
+    Y.wait_ge(S.sc, G)
+    Y.dma_start(T.h[:], T.hb[:]).then_inc(S.sh, 16)
+    for j, (ls, qs) in enumerate(((S.lv0, S.qv0), (S.lv1, S.qv1))):
+        V.wait_ge(ls, 16)
+        V.quantize_mx(T.w2q[:, 128 * j:128 * j + 128], T.w2s[:, 128 * j:128 * j + 128],
+                      T.w2b[:, TW * j:TW * j + TW]).then_inc(qs, 1)
+
+    E.wait_ge(S.qh, 1)
+    E.wait_ge(S.qv0, 1)
+    E.matmul_mx(T.yp[:, 0:NC], T.w2q[:, 0:128], T.w2s[:, 0:128], T.hq[:], T.hs[:], True, False)
+    arr = _count(topo.mask(port[(r + 1) % n], core))
+    E.wait_ge(S.qv1, 1)
+    E.wait_ge(S.cc, arr)
+    E.wait_ge(S.cs, arr)
+    E.matmul_mx(T.yp[:, 0:NC], T.w2q[:, 128:256], T.w2s[:, 128:256], T.nq[:], T.ns[:], False, True).then_inc(S.my, 1)
+    V.wait_ge(S.my, 1)
+    V.tensor_copy(T.yb[:], T.yp[:, 0:NC]).then_inc(S.cy, 1)
+    Y.wait_ge(S.cy, 1)
+    Y.dma_start(T.y[:], T.yb[:]).then_inc(S.sy, 16)
+    Y.wait_ge(S.sh, 16)
+    Y.wait_ge(S.sy, 16)
+
+
+def rank_program(g, core, T, topo):
+    cores, plane, partner, port = _plan(T, topo)
+    r = T.rank_of(core)
+    if r is not None:
+        _rank_program(g, core, T, topo, r, cores, plane, partner, port)
+    elif core in port:
+        _port_program(g, core, T, topo, port.index(core), cores, plane, partner, port)

@@ -1,10 +1,11 @@
 import math
 from concourse.bass import DstId, RemoteDMATransfer
-from concourse.mybir import dt, AluOpType, ActivationFunctionType
+from concourse.mybir import dt, AluOpType, AxisListType, ActivationFunctionType
 
 NC, G, EPS = 128, 4, 0.001
 TW = 4 * NC
 
+_COLS = ["ssA", "ssB", "hlA", "pA", "rA", "leB", "loB", "tB", "o", "c", "f", "f2", "a", "q", "iq", "rt", "g0"]
 SCRATCH = {
     "xb": ("sbuf", [128, TW], "bfloat16"),
     "w1b": ("sbuf", [128, G * TW], "bfloat16"),
@@ -18,21 +19,16 @@ SCRATCH = {
     "z": ("psum", [128, G * 512], "float32"),
     "yp": ("psum", [128, 512], "float32"),
     "sqr": ("sbuf", [128, G * NC], "float32"),
-    "ssA": ("sbuf", [128, 4], "float32"), "ssB": ("sbuf", [128, 4], "float32"),
-    "hlA": ("sbuf", [128, 4], "float32"), "hlB": ("sbuf", [128, 12], "float32"),
-    "leA": ("sbuf", [128, 4], "float32"), "loA": ("sbuf", [128, 4], "float32"),
-    "leB": ("sbuf", [128, 4], "float32"), "loB": ("sbuf", [128, 4], "float32"),
-    "tA": ("sbuf", [128, 4], "float32"), "tB": ("sbuf", [128, 4], "float32"),
-    "aA": ("sbuf", [128, 4], "float32"), "aB": ("sbuf", [128, 4], "float32"),
-    "ia": ("sbuf", [128, 4], "float32"), "rt": ("sbuf", [128, 4], "float32"),
-    "s0": ("sbuf", [128, 4], "float32"), "u": ("sbuf", [128, 4], "float32"),
-    "v": ("sbuf", [128, 4], "float32"), "s1": ("sbuf", [128, 4], "float32"),
+    "zf": ("sbuf", [128, G * NC], "float32"),
+    "hlB": ("sbuf", [128, 12], "float32"),
     "yb": ("sbuf", [128, NC], "float32"),
 }
-SEMAPHORES = (["lx", "lv0", "lv1", "qx", "qv0", "qv1", "qh", "my", "sqA", "sqB", "hA", "hB", "eA", "oA", "eB", "oB",
-               "cc", "cs", "locA", "locB", "locC", "ktA", "kaA", "kiA", "krA", "ktB", "kaB", "kiB", "krB",
-               "n0", "n1", "n2", "n3", "sc", "cy", "sh", "sy"]
-              + ["lw%d" % i for i in range(G)] + ["qw%d" % i for i in range(G)] + ["m%d" % i for i in range(G)])
+for _k in _COLS:
+    SCRATCH[_k] = ("sbuf", [128, 4], "float32")
+SEMAPHORES = (["lx", "lw0", "lw1", "lw3", "lv", "qx", "qv", "qh", "my", "sqA", "sqB", "hA", "hB", "eA", "eB", "oB",
+               "cc", "cs", "locA", "locB", "locC", "ko", "kc", "kf", "kf2", "ps", "k1", "ka", "kt", "kq", "ki", "kr",
+               "n0", "sc", "cy", "sh", "sy"]
+              + ["qw%d" % i for i in range(G)] + ["m%d" % i for i in range(G)])
 
 
 def _count(mask):
@@ -57,14 +53,14 @@ def _plan(T, topo):
         if r not in partner:
             q = left.pop(0)
             partner[r], partner[q] = q, r
-    port = []
+    px, py = [], []
     for r in range(n):
-        goals = (cores[partner[r]], cores[(r - 1) % n])
         cand = [k for k in range(topo.CHIPS * topo.CORES_PER_CHIP)
-                if topo.chip(k) == chips[r] and k not in cores and all(topo.may_write(k, d) for d in goals)]
+                if topo.chip(k) == chips[r] and k not in cores and all(topo.may_write(k, d) for d in cores)]
         cand.sort(key=lambda k: (topo.die(k) != topo.die(cores[r]), k))
-        port.append(cand[0])
-    return cores, plane, partner, port
+        px.append(cand[0])
+        py.append(cand[1])
+    return cores, plane, partner, px, py
 
 
 def _dst(topo, c):
@@ -80,61 +76,97 @@ def _send(g, topo, src, dst, out_ap, in_ap, rsem, lsem):
     return _count(m)
 
 
-def _port_program(g, core, T, topo, r, cores, plane, partner, port):
+def _place(plane, r, n):
+    P = plane[r]
+    Q = [q for q in range(n) if q not in P]
+    k, j = divmod(P.index(r), 2)
+    return P, Q, k, j, P[2 * k + 1 - j]
+
+
+def _helper_program(g, core, T, topo, r, is_x, cores, plane, partner, px, py):
     S = T.sem
-    mine, other = cores[r], cores[partner[r]]
-    lo = topo.mask(core, other)
-    hi = topo.mask(core, mine) & ~lo
-    due = 0
-    for q in plane[r]:
-        out = topo.mask(cores[q], port[[p for p in plane[r] if p != q][0]])
-        due += _count(topo.mask(cores[q], core) & ~out) if q == r else _count(out)
+    n = len(cores)
+    P, Q, k, j, pal = _place(plane, r, n)
+    mine = cores[r]
+    goal = cores[(r - 1) % n]
     left = 0
-    for land, w, asem, esem, osem, le, lo_buf in ((T.hlA, 1, S.hA, S.eA, S.oA, T.leA, T.loA),
-                                                  (T.hlB, 3, S.hB, S.eB, S.oB, T.leB, T.loB)):
-        srcs = [land[:, w * j:w * j + w] for j in range(len(plane[r]))]
-        g.wait_ge(asem, due)
+    due = _count(topo.mask(mine, core) & ~topo.mask(mine, px[pal])) + _count(topo.mask(cores[pal], core))
+    srcs = [T.hlA[:, 0:1], T.hlA[:, 1:2]]
+    g.wait_ge(S.hA, due)
+    if is_x:
+        other = cores[P[2 * (1 - k) + j]]
+        lo = topo.mask(core, other)
+        hi = topo.mask(core, mine) & ~lo
         g.remote_dma_fused([
-            RemoteDMATransfer(dst_ids=[_dst(topo, other)], dma_engine_mask=lo, remote_sem=osem, srcs=srcs,
-                              dsts=[lo_buf[:, 0:w]], alu_op=1),
-            RemoteDMATransfer(dst_ids=[_dst(topo, mine)], dma_engine_mask=hi, remote_sem=esem, srcs=srcs,
-                              dsts=[le[:, 0:w]], alu_op=1),
+            RemoteDMATransfer(dst_ids=[_dst(topo, other)], dma_engine_mask=lo, remote_sem=S.eA, srcs=srcs,
+                              dsts=[T.pA[:, 1:2]], alu_op=1),
+            RemoteDMATransfer(dst_ids=[_dst(topo, mine)], dma_engine_mask=hi, remote_sem=S.eA, srcs=srcs,
+                              dsts=[T.pA[:, 0:1]], alu_op=1),
         ], local_sem=S.locA)
         left += _count(lo) + _count(hi)
-    goal = cores[(r - 1) % len(cores)]
+    else:
+        goals = [cores[Q[2 * j]], cores[Q[2 * j + 1]]]
+        lo = topo.mask(core, goals[0])
+        g.remote_dma_fused([
+            RemoteDMATransfer(dst_ids=[_dst(topo, d) for d in goals], dma_engine_mask=lo, remote_sem=S.eA, srcs=srcs,
+                              dsts=[T.pA[:, 2 + k:3 + k] for _ in goals], alu_op=1),
+        ], local_sem=S.locA)
+        left += _count(lo)
     got = _count(topo.mask(mine, core))
-    g.wait_ge(S.cc, got)
-    left += _send(g, topo, core, goal, T.nq[:].bitcast(dt.uint8), T.nq[:].bitcast(dt.uint8), S.cc, S.locA)
-    g.wait_ge(S.cs, got)
-    left += _send(g, topo, core, goal, T.ns[:], T.ns[:], S.cs, S.locA)
+    if is_x:
+        other = cores[partner[r]]
+        lo = topo.mask(core, other)
+        hi = topo.mask(core, mine) & ~lo
+        due = 0
+        for q in P:
+            out = topo.mask(cores[q], px[[p for p in P if p != q][0]])
+            due += _count(topo.mask(cores[q], core) & ~out) if q == r else _count(out)
+        w = G - 1
+        srcs = [T.hlB[:, w * t:w * t + w] for t in range(len(P))]
+        g.wait_ge(S.hB, due)
+        g.remote_dma_fused([
+            RemoteDMATransfer(dst_ids=[_dst(topo, other)], dma_engine_mask=lo, remote_sem=S.oB, srcs=srcs,
+                              dsts=[T.loB[:, 0:w]], alu_op=1),
+            RemoteDMATransfer(dst_ids=[_dst(topo, mine)], dma_engine_mask=hi, remote_sem=S.eB, srcs=srcs,
+                              dsts=[T.leB[:, 0:w]], alu_op=1),
+        ], local_sem=S.locA)
+        left += _count(lo) + _count(hi)
+        g.wait_ge(S.cc, got)
+        left += _send(g, topo, core, goal, T.nq[:].bitcast(dt.uint8), T.nq[:].bitcast(dt.uint8), S.cc, S.locA)
+    else:
+        g.wait_ge(S.cs, got)
+        left += _send(g, topo, core, goal, T.ns[:], T.ns[:], S.cs, S.locA)
     g.wait_ge(S.locA, left)
 
 
-def _rank_program(g, core, T, topo, r, cores, plane, partner, port):
+def _rank_program(g, core, T, topo, r, cores, plane, partner, px, py):
     S = T.sem
     A, F = AluOpType, ActivationFunctionType
     n = len(cores)
     V, E, C, Y = g.vector, g.tensor, g.scalar, g.sync
-    my_port = port[r]
-    slot = plane[r].index(r)
-    away = [port[q] for q in plane[r] if q != r]
+    P, Q, k, j, pal = _place(plane, r, n)
+    X_, Y_ = px[r], py[r]
+    slot = P.index(r)
+    away = [px[q] for q in P if q != r]
     lo = topo.mask(core, away[0])
-    hi = topo.mask(core, my_port) & ~lo
+    hi = topo.mask(core, X_) & ~lo
+    part = _count(lo) + _count(hi)
 
     def w1t(i):
         return T.w1b[:, TW * i:TW * i + TW]
 
     Y.dma_start(T.xb[:], T.x[:]).then_inc(S.lx, 16)
-    for i in range(G):
-        q = C if i % 2 == 0 else Y
-        q.dma_start(w1t(i), T.w1[:, TW * i:TW * i + TW]).then_inc(S["lw%d" % i], 16)
+    C.dma_start(w1t(0), T.w1[:, 0:TW]).then_inc(S.lw0, 16)
+    Y.dma_start(T.w1b[:, TW:(G - 1) * TW], T.w1[:, TW:(G - 1) * TW]).then_inc(S.lw1, 16)
+    Y.dma_start(w1t(G - 1), T.w1[:, (G - 1) * TW:G * TW]).then_inc(S.lw3, 16)
+    came = [S.lw0] + [S.lw1] * (G - 2) + [S.lw3]
 
     V.wait_ge(S.lx, 16)
     V.quantize_mx(T.xq[:], T.xs[:], T.xb[:]).then_inc(S.qx, 1)
     E.wait_ge(S.qx, 1)
     for i in range(G):
         cq, cs = T.w1q[:, 128 * i:128 * i + 128], T.w1s[:, 128 * i:128 * i + 128]
-        V.wait_ge(S["lw%d" % i], 16)
+        V.wait_ge(came[i], 16)
         V.quantize_mx(cq, cs, w1t(i)).then_inc(S["qw%d" % i], 1)
         E.wait_ge(S["qw%d" % i], 1)
         E.matmul_mx(T.z[:, 512 * i:512 * i + NC], cq, cs, T.xq[:], T.xs[:], True, True).then_inc(S["m%d" % i], 1)
@@ -143,79 +175,94 @@ def _rank_program(g, core, T, topo, r, cores, plane, partner, port):
         C.activation(T.sqr[:, NC * i:NC * i + NC], T.z[:, 512 * i:512 * i + NC], F.Square,
                      scale=1.0 / math.sqrt(n * NC), accum_out=acc).then_inc(S.sqA if i == 0 else S.sqB, 1)
 
-    for src, land, w, ready, cnt, asem, lsem in ((T.ssA, T.hlA, 1, S.sqA, 1, S.hA, S.locA),
-                                                 (T.ssB, T.hlB, 3, S.sqB, G - 1, S.hB, S.locB)):
-        g.wait_ge(ready, cnt)
-        d = land[:, w * slot:w * slot + w]
-        g.remote_dma_fused([
-            RemoteDMATransfer(dst_ids=[_dst(topo, k) for k in away], dma_engine_mask=lo, remote_sem=asem,
-                              srcs=[src[:, 0:w]], dsts=[d for _ in away], alu_op=0),
-            RemoteDMATransfer(dst_ids=[_dst(topo, my_port)], dma_engine_mask=hi, remote_sem=asem,
-                              srcs=[src[:, 0:w]], dsts=[d], alu_op=0),
-        ], local_sem=lsem)
-    part = _count(lo) + _count(hi)
+    g.wait_ge(S.sqA, 1)
+    d = T.hlA[:, j:j + 1]
+    g.remote_dma_fused([
+        RemoteDMATransfer(dst_ids=[_dst(topo, px[pal]), _dst(topo, py[pal])], dma_engine_mask=lo, remote_sem=S.hA,
+                          srcs=[T.ssA[:, 0:1]], dsts=[d, d], alu_op=0),
+        RemoteDMATransfer(dst_ids=[_dst(topo, X_), _dst(topo, Y_)], dma_engine_mask=hi, remote_sem=S.hA,
+                          srcs=[T.ssA[:, 0:1]], dsts=[d, d], alu_op=0),
+    ], local_sem=S.locA)
+    w = G - 1
+    g.wait_ge(S.sqB, w)
+    d = T.hlB[:, w * slot:w * slot + w]
+    g.remote_dma_fused([
+        RemoteDMATransfer(dst_ids=[_dst(topo, t) for t in away], dma_engine_mask=lo, remote_sem=S.hB,
+                          srcs=[T.ssB[:, 0:w]], dsts=[d for _ in away], alu_op=0),
+        RemoteDMATransfer(dst_ids=[_dst(topo, X_)], dma_engine_mask=hi, remote_sem=S.hB,
+                          srcs=[T.ssB[:, 0:w]], dsts=[d], alu_op=0),
+    ], local_sem=S.locB)
 
-    p_lo = topo.mask(port[partner[r]], core)
-    p_hi = topo.mask(my_port, core) & ~topo.mask(my_port, cores[partner[r]])
-    for le, lob, t, a, c0, w, es, os_, kt, ka, ki, kr in (
-            (T.leA, T.loA, T.tA, T.aA, 0, 1, S.eA, S.oA, S.ktA, S.kaA, S.kiA, S.krA),
-            (T.leB, T.loB, T.tB, T.aB, 1, 3, S.eB, S.oB, S.ktB, S.kaB, S.kiB, S.krB)):
-        V.wait_ge(es, _count(p_hi))
-        V.tensor_scalar(t[:, 0:w], le[:, 0:w], EPS, None, A.add).then_inc(kt, 1)
-        V.wait_ge(os_, _count(p_lo))
-        V.wait_ge(kt, 1)
-        V.tensor_tensor(a[:, 0:w], t[:, 0:w], lob[:, 0:w], A.add).then_inc(ka, 1)
-        C.wait_ge(ka, 1)
-        C.activation(T.rt[:, c0:c0 + w], a[:, 0:w], F.Sqrt).then_inc(kr, 1)
-        V.wait_ge(ka, 1)
-        V.reciprocal(T.ia[:, c0:c0 + w], a[:, 0:w]).then_inc(ki, 1)
-
-    for k in (S.kiA, S.kiB, S.krA, S.krB):
-        V.wait_ge(k, 1)
-    V.tensor_tensor(T.s0[:], T.rt[:], T.ia[:], A.mult).then_inc(S.n0, 1)
-    V.wait_ge(S.n0, 1)
-    V.tensor_tensor(T.u[:], T.rt[:], T.s0[:], A.mult).then_inc(S.n1, 1)
-    V.wait_ge(S.n1, 1)
-    V.tensor_scalar(T.v[:], T.u[:], -0.5, 1.5, A.mult, A.add).then_inc(S.n2, 1)
-    V.wait_ge(S.n2, 1)
-    V.tensor_tensor(T.s1[:], T.s0[:], T.v[:], A.mult).then_inc(S.n3, 1)
-
-    V.wait_ge(S.n3, 1)
     V.wait_ge(S.sqA, 1)
-    V.wait_ge(S.sqB, G - 1)
-    C.wait_ge(S.n3, 1)
+    V.tensor_scalar(T.o[:, 0:1], T.ssA[:, 0:1], EPS, None, A.add).then_inc(S.ko, 1)
+    V.wait_ge(S.sqB, w)
+    V.tensor_scalar(T.o[:, 1:G], T.ssB[:, 0:w], EPS, None, A.add).then_inc(S.ko, 1)
+    C.wait_ge(S.ko, 2)
+    C.activation(T.c[:], T.o[:], F.Sqrt).then_inc(S.kc, 1)
+    V.wait_ge(S.kc, 1)
+    V.reciprocal(T.f[:], T.c[:]).then_inc(S.kf, 1)
+    V.wait_ge(S.kf, 1)
+    V.tensor_tensor(T.f2[:], T.f[:], T.f[:], A.mult).then_inc(S.kf2, 1)
+    C.wait_ge(S.kf, 1)
+    for b in range(G // 2, G):
+        C.activation(T.zf[:, NC * b:NC * b + NC], T.z[:, 512 * b:512 * b + NC], F.Identity,
+                     scale=T.f[:, b:b + 1]).then_inc(S.ps, 1)
+
+    dueA = (_count(topo.mask(X_, core) & ~topo.mask(X_, cores[pal]))
+            + _count(topo.mask(px[P[2 * (1 - k) + j]], core))
+            + sum(_count(topo.mask(py[Q[2 * t + k]], core)) for t in range(2)))
+    V.wait_ge(S.eA, dueA)
+    V.tensor_reduce(T.rA[:, 0:1], T.pA[:, 0:4], AxisListType.X, A.add).then_inc(S.k1, 1)
+    V.wait_ge(S.k1, 1)
+    V.tensor_scalar(T.a[:, 0:1], T.rA[:, 0:1], EPS, None, A.add).then_inc(S.ka, 1)
+    V.wait_ge(S.eB, _count(topo.mask(X_, core) & ~topo.mask(X_, cores[partner[r]])))
+    V.tensor_scalar(T.tB[:, 0:w], T.leB[:, 0:w], EPS, None, A.add).then_inc(S.kt, 1)
+    V.wait_ge(S.oB, _count(topo.mask(px[partner[r]], core)))
+    V.wait_ge(S.kt, 1)
+    V.tensor_tensor(T.a[:, 1:G], T.tB[:, 0:w], T.loB[:, 0:w], A.add).then_inc(S.ka, 1)
+
+    V.wait_ge(S.ka, 2)
+    V.wait_ge(S.kf2, 1)
+    V.tensor_tensor(T.q[:], T.a[:], T.f2[:], A.mult).then_inc(S.kq, 1)
+    C.wait_ge(S.kq, 1)
+    C.activation(T.rt[:], T.q[:], F.Sqrt).then_inc(S.kr, 1)
+    V.wait_ge(S.kq, 1)
+    V.reciprocal(T.iq[:], T.q[:]).then_inc(S.ki, 1)
+    V.wait_ge(S.ki, 1)
+    V.wait_ge(S.kr, 1)
+    V.tensor_tensor(T.g0[:], T.rt[:], T.iq[:], A.mult).then_inc(S.n0, 1)
+
+    V.wait_ge(S.n0, 1)
+    C.wait_ge(S.n0, 1)
+    C.wait_ge(S.ps, G - G // 2)
     for b in range(G):
-        out, zb, col = T.hb[:, b:TW:4], T.z[:, 512 * b:512 * b + NC], T.s1[:, b:b + 1]
+        out, col = T.hb[:, b:TW:4], T.g0[:, b:b + 1]
         if b < G // 2:
-            V.tensor_scalar(out, zb, col, None, A.mult).then_inc(S.sc, 1)
+            V.tensor_scalar(out, T.z[:, 512 * b:512 * b + NC], T.f[:, b:b + 1], col, A.mult, A.mult).then_inc(S.sc, 1)
         else:
-            C.activation(out, zb, F.Identity, scale=col).then_inc(S.sc, 1)
+            C.activation(out, T.zf[:, NC * b:NC * b + NC], F.Identity, scale=col).then_inc(S.sc, 1)
     V.wait_ge(S.sc, G)
     V.quantize_mx(T.hq[:], T.hs[:], T.hb[:]).then_inc(S.qh, 1)
 
     g.wait_ge(S.qh, 1)
-    gone = _send(g, topo, core, my_port, T.nq[:].bitcast(dt.uint8), T.hq[:].bitcast(dt.uint8), S.cc, S.locC)
-    gone += _send(g, topo, core, my_port, T.ns[:], T.hs[:], S.cs, S.locC)
+    gone = _send(g, topo, core, X_, T.nq[:].bitcast(dt.uint8), T.hq[:].bitcast(dt.uint8), S.cc, S.locC)
+    gone += _send(g, topo, core, Y_, T.ns[:], T.hs[:], S.cs, S.locC)
     g.wait_ge(S.locA, part)
 
     Y.wait_ge(S.locB, part)
-    Y.dma_start(T.w2b[:, 0:TW], T.w2[:, 0:TW]).then_inc(S.lv0, 16)
+    Y.dma_start(T.w2b[:], T.w2[:]).then_inc(S.lv, 16)
     Y.wait_ge(S.locC, gone)
-    Y.dma_start(T.w2b[:, TW:2 * TW], T.w2[:, TW:2 * TW]).then_inc(S.lv1, 16)
     Y.wait_ge(S.sc, G)
     Y.dma_start(T.h[:], T.hb[:]).then_inc(S.sh, 16)
-    for j, (ls, qs) in enumerate(((S.lv0, S.qv0), (S.lv1, S.qv1))):
-        V.wait_ge(ls, 16)
-        V.quantize_mx(T.w2q[:, 128 * j:128 * j + 128], T.w2s[:, 128 * j:128 * j + 128],
-                      T.w2b[:, TW * j:TW * j + TW]).then_inc(qs, 1)
+    V.wait_ge(S.lv, 16)
+    V.quantize_mx(T.w2q[:], T.w2s[:], T.w2b[:]).then_inc(S.qv, 1)
 
     E.wait_ge(S.qh, 1)
-    E.wait_ge(S.qv0, 1)
+    E.wait_ge(S.qv, 1)
     E.matmul_mx(T.yp[:, 0:NC], T.w2q[:, 0:128], T.w2s[:, 0:128], T.hq[:], T.hs[:], True, False)
-    arr = _count(topo.mask(port[(r + 1) % n], core))
-    E.wait_ge(S.qv1, 1)
-    E.wait_ge(S.cc, arr)
-    E.wait_ge(S.cs, arr)
+    nxt = (r + 1) % n
+    E.wait_ge(S.cc, _count(topo.mask(px[nxt], core)))
+    E.wait_ge(S.cs, _count(topo.mask(py[nxt], core)))
     E.matmul_mx(T.yp[:, 0:NC], T.w2q[:, 128:256], T.w2s[:, 128:256], T.nq[:], T.ns[:], False, True).then_inc(S.my, 1)
     V.wait_ge(S.my, 1)
     V.tensor_copy(T.yb[:], T.yp[:, 0:NC]).then_inc(S.cy, 1)
@@ -226,9 +273,11 @@ def _rank_program(g, core, T, topo, r, cores, plane, partner, port):
 
 
 def rank_program(g, core, T, topo):
-    cores, plane, partner, port = _plan(T, topo)
+    cores, plane, partner, px, py = _plan(T, topo)
     r = T.rank_of(core)
     if r is not None:
-        _rank_program(g, core, T, topo, r, cores, plane, partner, port)
-    elif core in port:
-        _port_program(g, core, T, topo, port.index(core), cores, plane, partner, port)
+        _rank_program(g, core, T, topo, r, cores, plane, partner, px, py)
+    elif core in px:
+        _helper_program(g, core, T, topo, px.index(core), True, cores, plane, partner, px, py)
+    elif core in py:
+        _helper_program(g, core, T, topo, py.index(core), False, cores, plane, partner, px, py)

import math
from concourse.bass import DstId, RemoteDMATransfer
from concourse.mybir import dt, AluOpType, AxisListType, ActivationFunctionType

NC, G, EPS = 128, 4, 0.001
TW = 4 * NC

_COLS = ["ssA", "ssB", "hlA", "pA", "rA", "leB", "loB", "tB", "o", "c", "f", "f2", "a", "q", "iq", "rt", "g0"]
SCRATCH = {
    "xb": ("sbuf", [128, TW], "bfloat16"),
    "w1b": ("sbuf", [128, G * TW], "bfloat16"),
    "w2b": ("sbuf", [128, 2 * TW], "bfloat16"),
    "hb": ("sbuf", [128, TW], "bfloat16"),
    "xq": ("sbuf", [128, NC], "float8_e4m3fn_x4"), "xs": ("sbuf", [128, NC], "uint8"),
    "w1q": ("sbuf", [128, G * 128], "float8_e4m3fn_x4"), "w1s": ("sbuf", [128, G * 128], "uint8"),
    "w2q": ("sbuf", [128, 2 * 128], "float8_e4m3fn_x4"), "w2s": ("sbuf", [128, 2 * 128], "uint8"),
    "hq": ("sbuf", [128, NC], "float8_e4m3fn_x4"), "hs": ("sbuf", [128, NC], "uint8"),
    "nq": ("sbuf", [128, NC], "float8_e4m3fn_x4"), "ns": ("sbuf", [128, NC], "uint8"),
    "z": ("psum", [128, G * 512], "float32"),
    "yp": ("psum", [128, 512], "float32"),
    "sqr": ("sbuf", [128, G * NC], "float32"),
    "zf": ("sbuf", [128, G * NC], "float32"),
    "hlB": ("sbuf", [128, 12], "float32"),
    "yb": ("sbuf", [128, NC], "float32"),
}
for _k in _COLS:
    SCRATCH[_k] = ("sbuf", [128, 4], "float32")
SEMAPHORES = (["lx", "lw0", "lw1", "lw3", "lv", "qx", "qv", "qh", "my", "sqA", "sqB", "hA", "hB", "eA", "eB", "oB",
               "cc", "cs", "locA", "locB", "locC", "ko", "kc", "kf", "kf2", "ps", "k1", "ka", "kt", "kq", "ki", "kr",
               "n0", "sc", "cy", "sh", "sy"]
              + ["qw%d" % i for i in range(G)] + ["m%d" % i for i in range(G)])


def _count(mask):
    return bin(mask).count("1")


def _plan(T, topo):
    cores = [int(c) for c in T.cores]
    n = len(cores)
    chips = [topo.chip(c) for c in cores]
    near = [r for r in range(n) if r == 0 or topo.same_plane(chips[0], chips[r])]
    far = [r for r in range(n) if r not in near]
    plane = [near if r in near else far for r in range(n)]
    partner, left = {}, list(far)
    for r in near:
        for q in left:
            if topo.mates(chips[r], chips[q]):
                partner[r], partner[q] = q, r
                left.remove(q)
                break
    for r in near:
        if r not in partner:
            q = left.pop(0)
            partner[r], partner[q] = q, r
    px, py = [], []
    for r in range(n):
        cand = [k for k in range(topo.CHIPS * topo.CORES_PER_CHIP)
                if topo.chip(k) == chips[r] and k not in cores and all(topo.may_write(k, d) for d in cores)]
        cand.sort(key=lambda k: (topo.die(k) != topo.die(cores[r]), k))
        px.append(cand[0])
        py.append(cand[1])
    return cores, plane, partner, px, py


def _dst(topo, c):
    rid, pid, _ = topo.addr(c)
    return DstId(rid=rid, pnc=pid)


def _send(g, topo, src, dst, out_ap, in_ap, rsem, lsem):
    rid, pid, _ = topo.addr(dst)
    m = topo.mask(src, dst)
    g.remote_dma(out_ap=out_ap, in_ap=in_ap, remote_sem=rsem, local_sem=lsem, pid=pid, routing_id=rid,
                 dma_engine_mask=m)
    return _count(m)


def _place(plane, r, n):
    P = plane[r]
    Q = [q for q in range(n) if q not in P]
    k, j = divmod(P.index(r), 2)
    return P, Q, k, j, P[2 * k + 1 - j]


def _helper_program(g, core, T, topo, r, is_x, cores, plane, partner, px, py):
    S = T.sem
    n = len(cores)
    P, Q, k, j, pal = _place(plane, r, n)
    mine = cores[r]
    goal = cores[(r - 1) % n]
    left = 0
    due = _count(topo.mask(mine, core) & ~topo.mask(mine, px[pal])) + _count(topo.mask(cores[pal], core))
    srcs = [T.hlA[:, 0:1], T.hlA[:, 1:2]]
    g.wait_ge(S.hA, due)
    if is_x:
        other = cores[P[2 * (1 - k) + j]]
        lo = topo.mask(core, other)
        hi = topo.mask(core, mine) & ~lo
        g.remote_dma_fused([
            RemoteDMATransfer(dst_ids=[_dst(topo, other)], dma_engine_mask=lo, remote_sem=S.eA, srcs=srcs,
                              dsts=[T.pA[:, 1:2]], alu_op=1),
            RemoteDMATransfer(dst_ids=[_dst(topo, mine)], dma_engine_mask=hi, remote_sem=S.eA, srcs=srcs,
                              dsts=[T.pA[:, 0:1]], alu_op=1),
        ], local_sem=S.locA)
        left += _count(lo) + _count(hi)
    else:
        goals = [cores[Q[2 * j]], cores[Q[2 * j + 1]]]
        lo = topo.mask(core, goals[0])
        g.remote_dma_fused([
            RemoteDMATransfer(dst_ids=[_dst(topo, d) for d in goals], dma_engine_mask=lo, remote_sem=S.eA, srcs=srcs,
                              dsts=[T.pA[:, 2 + k:3 + k] for _ in goals], alu_op=1),
        ], local_sem=S.locA)
        left += _count(lo)
    got = _count(topo.mask(mine, core))
    if is_x:
        other = cores[partner[r]]
        lo = topo.mask(core, other)
        hi = topo.mask(core, mine) & ~lo
        due = 0
        for q in P:
            out = topo.mask(cores[q], px[[p for p in P if p != q][0]])
            due += _count(topo.mask(cores[q], core) & ~out) if q == r else _count(out)
        w = G - 1
        srcs = [T.hlB[:, w * t:w * t + w] for t in range(len(P))]
        g.wait_ge(S.hB, due)
        g.remote_dma_fused([
            RemoteDMATransfer(dst_ids=[_dst(topo, other)], dma_engine_mask=lo, remote_sem=S.oB, srcs=srcs,
                              dsts=[T.loB[:, 0:w]], alu_op=1),
            RemoteDMATransfer(dst_ids=[_dst(topo, mine)], dma_engine_mask=hi, remote_sem=S.eB, srcs=srcs,
                              dsts=[T.leB[:, 0:w]], alu_op=1),
        ], local_sem=S.locA)
        left += _count(lo) + _count(hi)
        g.wait_ge(S.cc, got)
        left += _send(g, topo, core, goal, T.nq[:].bitcast(dt.uint8), T.nq[:].bitcast(dt.uint8), S.cc, S.locA)
    else:
        g.wait_ge(S.cs, got)
        left += _send(g, topo, core, goal, T.ns[:], T.ns[:], S.cs, S.locA)
    g.wait_ge(S.locA, left)


def _rank_program(g, core, T, topo, r, cores, plane, partner, px, py):
    S = T.sem
    A, F = AluOpType, ActivationFunctionType
    n = len(cores)
    V, E, C, Y = g.vector, g.tensor, g.scalar, g.sync
    P, Q, k, j, pal = _place(plane, r, n)
    X_, Y_ = px[r], py[r]
    slot = P.index(r)
    away = [px[q] for q in P if q != r]
    lo = topo.mask(core, away[0])
    hi = topo.mask(core, X_) & ~lo
    part = _count(lo) + _count(hi)

    def w1t(i):
        return T.w1b[:, TW * i:TW * i + TW]

    Y.dma_start(T.xb[:], T.x[:]).then_inc(S.lx, 16)
    C.dma_start(w1t(0), T.w1[:, 0:TW]).then_inc(S.lw0, 16)
    Y.dma_start(T.w1b[:, TW:(G - 1) * TW], T.w1[:, TW:(G - 1) * TW]).then_inc(S.lw1, 16)
    Y.dma_start(w1t(G - 1), T.w1[:, (G - 1) * TW:G * TW]).then_inc(S.lw3, 16)
    came = [S.lw0] + [S.lw1] * (G - 2) + [S.lw3]

    V.wait_ge(S.lx, 16)
    V.quantize_mx(T.xq[:], T.xs[:], T.xb[:]).then_inc(S.qx, 1)
    E.wait_ge(S.qx, 1)
    for i in range(G):
        cq, cs = T.w1q[:, 128 * i:128 * i + 128], T.w1s[:, 128 * i:128 * i + 128]
        V.wait_ge(came[i], 16)
        V.quantize_mx(cq, cs, w1t(i)).then_inc(S["qw%d" % i], 1)
        E.wait_ge(S["qw%d" % i], 1)
        E.matmul_mx(T.z[:, 512 * i:512 * i + NC], cq, cs, T.xq[:], T.xs[:], True, True).then_inc(S["m%d" % i], 1)
        C.wait_ge(S["m%d" % i], 1)
        acc = T.ssA[:, 0:1] if i == 0 else T.ssB[:, i - 1:i]
        C.activation(T.sqr[:, NC * i:NC * i + NC], T.z[:, 512 * i:512 * i + NC], F.Square,
                     scale=1.0 / math.sqrt(n * NC), accum_out=acc).then_inc(S.sqA if i == 0 else S.sqB, 1)

    g.wait_ge(S.sqA, 1)
    d = T.hlA[:, j:j + 1]
    g.remote_dma_fused([
        RemoteDMATransfer(dst_ids=[_dst(topo, px[pal]), _dst(topo, py[pal])], dma_engine_mask=lo, remote_sem=S.hA,
                          srcs=[T.ssA[:, 0:1]], dsts=[d, d], alu_op=0),
        RemoteDMATransfer(dst_ids=[_dst(topo, X_), _dst(topo, Y_)], dma_engine_mask=hi, remote_sem=S.hA,
                          srcs=[T.ssA[:, 0:1]], dsts=[d, d], alu_op=0),
    ], local_sem=S.locA)
    w = G - 1
    g.wait_ge(S.sqB, w)
    d = T.hlB[:, w * slot:w * slot + w]
    g.remote_dma_fused([
        RemoteDMATransfer(dst_ids=[_dst(topo, t) for t in away], dma_engine_mask=lo, remote_sem=S.hB,
                          srcs=[T.ssB[:, 0:w]], dsts=[d for _ in away], alu_op=0),
        RemoteDMATransfer(dst_ids=[_dst(topo, X_)], dma_engine_mask=hi, remote_sem=S.hB,
                          srcs=[T.ssB[:, 0:w]], dsts=[d], alu_op=0),
    ], local_sem=S.locB)

    V.wait_ge(S.sqA, 1)
    V.tensor_scalar(T.o[:, 0:1], T.ssA[:, 0:1], EPS, None, A.add).then_inc(S.ko, 1)
    V.wait_ge(S.sqB, w)
    V.tensor_scalar(T.o[:, 1:G], T.ssB[:, 0:w], EPS, None, A.add).then_inc(S.ko, 1)
    C.wait_ge(S.ko, 2)
    C.activation(T.c[:], T.o[:], F.Sqrt).then_inc(S.kc, 1)
    V.wait_ge(S.kc, 1)
    V.reciprocal(T.f[:], T.c[:]).then_inc(S.kf, 1)
    V.wait_ge(S.kf, 1)
    V.tensor_tensor(T.f2[:], T.f[:], T.f[:], A.mult).then_inc(S.kf2, 1)
    C.wait_ge(S.kf, 1)
    for b in range(G // 2, G):
        C.activation(T.zf[:, NC * b:NC * b + NC], T.z[:, 512 * b:512 * b + NC], F.Identity,
                     scale=T.f[:, b:b + 1]).then_inc(S.ps, 1)

    dueA = (_count(topo.mask(X_, core) & ~topo.mask(X_, cores[pal]))
            + _count(topo.mask(px[P[2 * (1 - k) + j]], core))
            + sum(_count(topo.mask(py[Q[2 * t + k]], core)) for t in range(2)))
    V.wait_ge(S.eA, dueA)
    V.tensor_reduce(T.rA[:, 0:1], T.pA[:, 0:4], AxisListType.X, A.add).then_inc(S.k1, 1)
    V.wait_ge(S.k1, 1)
    V.tensor_scalar(T.a[:, 0:1], T.rA[:, 0:1], EPS, None, A.add).then_inc(S.ka, 1)
    V.wait_ge(S.eB, _count(topo.mask(X_, core) & ~topo.mask(X_, cores[partner[r]])))
    V.tensor_scalar(T.tB[:, 0:w], T.leB[:, 0:w], EPS, None, A.add).then_inc(S.kt, 1)
    V.wait_ge(S.oB, _count(topo.mask(px[partner[r]], core)))
    V.wait_ge(S.kt, 1)
    V.tensor_tensor(T.a[:, 1:G], T.tB[:, 0:w], T.loB[:, 0:w], A.add).then_inc(S.ka, 1)

    V.wait_ge(S.ka, 2)
    V.wait_ge(S.kf2, 1)
    V.tensor_tensor(T.q[:], T.a[:], T.f2[:], A.mult).then_inc(S.kq, 1)
    C.wait_ge(S.kq, 1)
    C.activation(T.rt[:], T.q[:], F.Sqrt).then_inc(S.kr, 1)
    V.wait_ge(S.kq, 1)
    V.reciprocal(T.iq[:], T.q[:]).then_inc(S.ki, 1)
    V.wait_ge(S.ki, 1)
    V.wait_ge(S.kr, 1)
    V.tensor_tensor(T.g0[:], T.rt[:], T.iq[:], A.mult).then_inc(S.n0, 1)

    V.wait_ge(S.n0, 1)
    C.wait_ge(S.n0, 1)
    C.wait_ge(S.ps, G - G // 2)
    for b in range(G):
        out, col = T.hb[:, b:TW:4], T.g0[:, b:b + 1]
        if b < G // 2:
            V.tensor_scalar(out, T.z[:, 512 * b:512 * b + NC], T.f[:, b:b + 1], col, A.mult, A.mult).then_inc(S.sc, 1)
        else:
            C.activation(out, T.zf[:, NC * b:NC * b + NC], F.Identity, scale=col).then_inc(S.sc, 1)
    V.wait_ge(S.sc, G)
    V.quantize_mx(T.hq[:], T.hs[:], T.hb[:]).then_inc(S.qh, 1)

    g.wait_ge(S.qh, 1)
    gone = _send(g, topo, core, X_, T.nq[:].bitcast(dt.uint8), T.hq[:].bitcast(dt.uint8), S.cc, S.locC)
    gone += _send(g, topo, core, Y_, T.ns[:], T.hs[:], S.cs, S.locC)
    g.wait_ge(S.locA, part)

    Y.wait_ge(S.locB, part)
    Y.dma_start(T.w2b[:], T.w2[:]).then_inc(S.lv, 16)
    Y.wait_ge(S.locC, gone)
    Y.wait_ge(S.sc, G)
    Y.dma_start(T.h[:], T.hb[:]).then_inc(S.sh, 16)
    V.wait_ge(S.lv, 16)
    V.quantize_mx(T.w2q[:], T.w2s[:], T.w2b[:]).then_inc(S.qv, 1)

    E.wait_ge(S.qh, 1)
    E.wait_ge(S.qv, 1)
    E.matmul_mx(T.yp[:, 0:NC], T.w2q[:, 0:128], T.w2s[:, 0:128], T.hq[:], T.hs[:], True, False)
    nxt = (r + 1) % n
    E.wait_ge(S.cc, _count(topo.mask(px[nxt], core)))
    E.wait_ge(S.cs, _count(topo.mask(py[nxt], core)))
    E.matmul_mx(T.yp[:, 0:NC], T.w2q[:, 128:256], T.w2s[:, 128:256], T.nq[:], T.ns[:], False, True).then_inc(S.my, 1)
    V.wait_ge(S.my, 1)
    V.tensor_copy(T.yb[:], T.yp[:, 0:NC]).then_inc(S.cy, 1)
    Y.wait_ge(S.cy, 1)
    Y.dma_start(T.y[:], T.yb[:]).then_inc(S.sy, 16)
    Y.wait_ge(S.sh, 16)
    Y.wait_ge(S.sy, 16)


def rank_program(g, core, T, topo):
    cores, plane, partner, px, py = _plan(T, topo)
    r = T.rank_of(core)
    if r is not None:
        _rank_program(g, core, T, topo, r, cores, plane, partner, px, py)
    elif core in px:
        _helper_program(g, core, T, topo, px.index(core), True, cores, plane, partner, px, py)
    elif core in py:
        _helper_program(g, core, T, topo, py.index(core), False, cores, plane, partner, px, py)
